import numpy as np
import ml_dtypes


def mxq(x, axis, fmt="e4m3"):
    dtype, down = {"e4m3": (ml_dtypes.float8_e4m3fn, 7), "e5m2": (ml_dtypes.float8_e5m2, 14)}[fmt]
    v = np.moveaxis(np.asarray(x, np.float32).astype(ml_dtypes.bfloat16).astype(np.float64), axis, -1)
    blocks = v.reshape(v.shape[:-1] + (-1, 32))
    amax = np.abs(blocks).max(-1, keepdims=True)
    byte = np.maximum(np.where(amax > 0, np.frexp(amax)[1] - 1 + 127, 0) - down, 1)
    scale = np.exp2(byte - 127.0)
    codes = (blocks / scale).astype(np.float32).astype(dtype).astype(np.float64)
    return np.moveaxis((codes * scale).reshape(v.shape), -1, axis)


WIDE = False


def mx_kscale(k):
    if not WIDE:
        return np.ones(k)
    levels = np.array([10, -10, 5, -5, 0])
    if k % 512:
        return np.exp2(np.random.permutation(np.resize(levels, k // 32))).repeat(32)
    a = np.empty((k // 512, 16))
    for p in range(k // 512):
        a[p, :8] = np.random.permutation(np.resize(levels, 8))
        for g in range(8):
            far = levels[np.abs(levels - a[p, g]) >= 10]
            a[p, g + 8] = far[np.random.randint(len(far))]
    return np.exp2(a.ravel()).repeat(32)


def f64(x):
    return np.asarray(x).astype(np.float64)


def striped(idx):
    return np.tile(idx.reshape(-1, 16).T, (8, 1)).astype(np.uint16)


def unstriped(offs):
    return offs[:16].T.reshape(-1).astype(np.int64)


def striped8(idx):
    return np.concatenate([x.reshape(-1, 16).T for x in idx]).astype(np.uint16)


def runs(offs, k):
    lists = np.stack([offs[16 * r : 16 * r + 16].T.reshape(-1) for r in range(8)]).astype(np.int64)
    return lists[np.arange(k) % 512 // 64]


def pack_weight(w):
    k, n = w.shape
    w = f64(np.asarray(w, np.float32).astype(ml_dtypes.bfloat16)).reshape(k // 32, 32, n)
    amax = np.abs(w).max(1)
    byte = np.clip(np.where(amax > 0, np.frexp(amax)[1] - 1 + 127 - 7, 1), 1, 254)
    scaled = (w * np.exp2(127.0 - byte)[:, None, :]).reshape(k, n).astype(np.float32)
    words = np.ascontiguousarray(scaled.reshape(k // 512, 128, 4, n).transpose(0, 1, 3, 2)).astype(ml_dtypes.float8_e4m3fn).view(np.uint8)
    return words, np.ascontiguousarray(byte.astype(np.uint8).reshape(k // 512, 16, n))


def unpack_weight(words, scales):
    g, p, n, _ = words.shape
    vals = np.ascontiguousarray(words).view(ml_dtypes.float8_e4m3fn).astype(np.float64) * np.repeat(np.exp2(scales.astype(np.float64) - 127.0), 8, axis=1)[..., None]
    return vals.transpose(0, 1, 3, 2).reshape(g * 512, n)

def planes(y):
    n, m = y.shape
    v = y.astype(np.float32).astype(ml_dtypes.bfloat16).astype(np.float64).reshape(n // 32, 32, m)
    top = np.abs(v).max(1)
    byte = np.clip(np.where(top > 0, np.frexp(top)[1] - 1 + 127 - 7, 1), 1, 254)
    codes = (v * np.exp2(127.0 - byte)[:, None, :]).reshape(n, m).astype(np.float32).astype(ml_dtypes.float8_e4m3fn).view(np.uint8)
    words = codes.reshape(n // 512, 128, 4, m).transpose(0, 1, 3, 2)
    return np.ascontiguousarray(words), np.ascontiguousarray(byte.astype(np.uint8).reshape(n // 512, 16, m))


K, T, S, G, H = 512, 1024, 512, 2048, 512


def setup_inputs():
    n = np.random.standard_normal
    s = mx_kscale(K)[:, None]
    packed_xT = pack_weight(n((K, T)) * s)
    packed_dT = pack_weight(n((K, G)) / s)
    return {
        "x_words": packed_xT[0],
        "x_scales": packed_xT[1],
        "d_words": packed_dT[0],
        "d_scales": packed_dT[1],
        "tau": np.random.uniform(0.3, 0.9, (H, 1)).astype(np.float32),
        "tau2": np.random.uniform(0.3, 0.9, (H, 1)).astype(np.float32),
        "gs": (np.random.uniform(0.5, 1.5, (K, 1)) * s).astype(np.float32),
        "tau3": np.random.uniform(0.2, 0.6, (H, 1)).astype(np.float32),
        "tau4": np.random.uniform(0.6, 1.0, (H, 1)).astype(np.float32),
        "offs": striped(np.random.permutation(T)[:S]),
        "k1": striped8(np.random.randint(0, G, (8, H))),
        "n1": striped8(np.stack([np.random.permutation(S) for _ in range(8)])),
        "n2": striped8(np.stack([np.random.permutation(S) for _ in range(8)])),
        "k2": striped8(np.random.randint(0, G, (8, H))),
        "n3": striped8(np.stack([np.random.permutation(S) for _ in range(8)])),
        "n4": striped8(np.stack([np.random.permutation(S) for _ in range(8)])),
    }


def reference(x_words, x_scales, d_words, d_scales, tau, tau2, gs, tau3, tau4, offs, k1, n1, n2, k2, n3, n4):
    d_k2 = unpack_weight(d_words, d_scales)[np.arange(K)[:, None], runs(k2, K)]
    d_k1 = unpack_weight(d_words, d_scales)[np.arange(K)[:, None], runs(k1, K)]
    xq = unpack_weight(x_words, x_scales)[:, unstriped(offs)]
    h = 0.0625 * (d_k1.T @ xq)
    top = h.max(axis=1, keepdims=True)
    ea = np.exp(f64(tau) * (h[np.arange(H)[:, None], runs(n1, H)] - top))
    ea2 = np.exp(f64(tau2) * (h[np.arange(H)[:, None], runs(n2, H)] - top))
    z = f64(gs) * (0.5 * h + np.log((ea + 0.25) / (ea2 + 0.25)))
    h2 = 0.0625 * ((d_k2.T @ mxq(z, 0, "e4m3")))
    top2 = h2.max(axis=1, keepdims=True)
    ea3 = np.exp(f64(tau3) * (h2[np.arange(H)[:, None], runs(n3, H)] - top2))
    ea4 = np.exp(f64(tau4) * (h2[np.arange(H)[:, None], runs(n4, H)] - top2))
    out_0 = 3.0 * (ea3 - ea4)
    return (out_0,) + planes(out_0)

@@ -1,0 +1,216 @@
+from contextlib import ExitStack
+
+import concourse.mybir as mybir
+
+F32 = mybir.dt.float32
+BF16 = mybir.dt.bfloat16
+I32 = mybir.dt.int32
+U32 = mybir.dt.uint32
+U16 = mybir.dt.uint16
+U8 = mybir.dt.uint8
+FP8X4 = mybir.dt.float8_e4m3fn_x4
+ALU = mybir.AluOpType
+ACT = mybir.ActivationFunctionType
+
+P = 128
+PACK = 4
+K, T, S, G, H = 512, 1024, 512, 2048, 512
+FLOPS = 2 * 2 * K * H * S
+
+OUT_PIECES = [(0, 256), (256, 384), (384, 512)]
+HALVES = [(0, 256), (256, 512)]
+
+
+def tile_picked_codeeosetw_none_po_kernel(
+    tc, x_words, x_scales, d_words, d_scales, tau, tau2, gs, tau3, tau4,
+    offs, k1, n1, n2, k2, n3, n4, out_0, out_1, out_2,
+):
+    nc = tc.nc
+    with ExitStack() as ctx:
+        keep = ctx.enter_context(tc.tile_pool(name="keep", bufs=1))
+        work = ctx.enter_context(tc.tile_pool(name="work", bufs=1))
+        psum = ctx.enter_context(tc.psum_pool(name="psum", bufs=1))
+
+        def load_list(src, name):
+            tile = keep.tile([P, S // 16], U16, name=name)
+            nc.sync.dma_start(tile[:], src)
+            return tile
+
+        def load_rows(src, name):
+            tile = keep.tile([P, PACK], F32, name=name)
+            nc.gpsimd.dma_start(tile[:], src.rearrange("(p t) o -> p (t o)", t=PACK))
+            return tile
+
+        ds_tab = keep.tile([P, G], U8, name="ds_tab")
+        xs_tab = keep.tile([P, T], U8, name="xs_tab")
+        nc.vector.memset(ds_tab[:].bitcast(I32), 0)
+        nc.vector.memset(xs_tab[:].bitcast(I32), 0)
+        k1_sb = load_list(k1, "k1_sb")
+        ds_rows = d_scales[0].bitcast(I32)
+        for e in range(2):
+            nc.scalar.dma_start(ds_tab[e:P:16, :].bitcast(I32), ds_rows[e:16:2, :])
+        offs_sb = load_list(offs, "offs_sb")
+        n1_sb = load_list(n1, "n1_sb")
+        n2_sb = load_list(n2, "n2_sb")
+        xw_tab = keep.tile([P, T], I32, name="xw_tab")
+        nc.sync.dma_start(xw_tab[:], x_words[0].rearrange("p n t -> p (n t)").bitcast(I32))
+        dw_tab = keep.tile([P, G], I32, name="dw_tab")
+        nc.sync.dma_start(dw_tab[:], d_words[0].rearrange("p n t -> p (n t)").bitcast(I32))
+        tau_sb = load_rows(tau, "tau_sb")
+        tau2_sb = load_rows(tau2, "tau2_sb")
+        xs_rows = x_scales[0].bitcast(I32)
+        for r in range(4):
+            queue = nc.scalar if r < 2 else nc.gpsimd
+            queue.dma_start(xs_tab[r:P:32, :].bitcast(I32), xs_rows[r:16:4, :])
+        gs_sb = load_rows(gs, "gs_sb")
+        tau3_sb = load_rows(tau3, "tau3_sb")
+        tau4_sb = load_rows(tau4, "tau4_sb")
+        k2_sb = load_list(k2, "k2_sb")
+        n3_sb = load_list(n3, "n3_sb")
+        n4_sb = load_list(n4, "n4_sb")
+
+        neg12 = keep.tile([P, PACK, 2], F32, name="neg12")
+        nc.scalar.activation(neg12[:, :, 0], tau_sb[:], ACT.Copy, scale=-1.0)
+        nc.scalar.activation(neg12[:, :, 1], tau2_sb[:], ACT.Copy, scale=-1.0)
+        neg34 = keep.tile([P, PACK, 2], F32, name="neg34")
+        nc.gpsimd.tensor_scalar(neg34[:, :, 0], tau3_sb[:], -1.0, 0.0, ALU.mult, ALU.add)
+        nc.gpsimd.tensor_scalar(neg34[:, :, 1], tau4_sb[:], -1.0, 0.0, ALU.mult, ALU.add)
+
+        def pick(table, codes, dtype, tag, name):
+            picked = work.tile([P, S], dtype, name=name, tag=tag, align_bytes=64)
+            nc.vector.tensor_copy(picked[:], table.indirect(codes[:]))
+            return picked
+
+        def deal(dealt, picked, ts):
+            nc.vector.tensor_copy(
+                dealt.rearrange("p (t m) -> p m t", t=PACK)[:, :, ts],
+                picked.rearrange("p (m t) -> p m t", t=PACK)[:, :, ts],
+            )
+
+        def place_scales(picked, queue, name):
+            dealt = work.tile([P, H], U8, name=name, align_bytes=64)
+            deal(dealt[:], picked[:], slice(0, PACK))
+            for e in range(2):
+                queue.dma_start(dealt[2 + e : P : 32, :].bitcast(I32), dealt[16 + e : P : 32, :].bitcast(I32))
+            return dealt
+
+        def multiply(bank, cols, t, w, ws, a, a_s):
+            m = slice(t * P, (t + 1) * P)
+            nc.tensor.matmul_mx(
+                out=bank[:, cols], lhsT=w[:, m].bitcast(FP8X4), lhsT_scale=ws[:, m],
+                rhs=a[:, cols].bitcast(FP8X4), rhs_scale=a_s[:, cols], start=True, stop=True,
+            )
+
+        def leave_bank(bank, t, neg, name):
+            rows = work.tile([P, S], F32, name="%s%d" % (name, t))
+            top = work.tile([P, 1], F32, name="%s_top%d" % (name, t))
+            nc.vector.tensor_scalar(rows[:], bank[:], 0.0625, None, ALU.mult, ALU.max, accum_out=top[:])
+            bias = work.tile([P, 2], F32, name="%s_bias%d" % (name, t))
+            nc.vector.tensor_scalar(bias[:], neg[:, t, :], top[:], None, ALU.mult)
+            return rows, bias
+
+        def fetch_exp(dst, rows, places, lo, hi, rate, bias):
+            nc.scalar.activation(
+                dst, rows[:].indirect(places[:, lo // 16 : hi // 16]), ACT.Exp, bias=bias, scale=rate,
+            )
+
+        dw_words = dw_tab[:].bitcast(U32)
+        d1s = pick(ds_tab[:], k1_sb, U8, "scales_d", "d1s")
+        xw = pick(xw_tab[:].bitcast(U32), offs_sb, U32, "words_x", "xw")
+        w1s = place_scales(d1s, nc.sync, "w1s")
+        d1w = pick(dw_words, k1_sb, U32, "words_d", "d1w")
+        xs = pick(xs_tab[:], offs_sb, U8, "scales_x", "xs")
+        w1 = work.tile([P, H], I32, name="w1", align_bytes=64)
+        deal(w1[:], d1w[:].bitcast(I32), slice(0, 1))
+        deal(w1[:], d1w[:].bitcast(I32), slice(1, PACK))
+
+        banks1 = [psum.tile([P, S], F32, name="bank1_%d" % t) for t in range(PACK)]
+        for t in range(PACK):
+            multiply(banks1[t], slice(0, S), t, w1, w1s, xw, xs)
+        layer1 = [leave_bank(banks1[t], t, neg12, "h") for t in range(PACK)]
+
+        ea = work.tile([P, PACK, 2, S], F32, name="ea")
+        for t in range(PACK):
+            h, bias = layer1[t]
+            for lo, hi in HALVES:
+                fetch_exp(ea[:, t, 0, lo:hi], h, n1_sb, lo, hi, tau_sb[:, t : t + 1], bias[:, 0:1])
+                fetch_exp(ea[:, t, 1, lo:hi], h, n2_sb, lo, hi, tau2_sb[:, t : t + 1], bias[:, 1:2])
+
+        d2s = pick(ds_tab[:], k2_sb, U8, "scales_x", "d2s")
+        d2w = pick(dw_words, k2_sb, U32, "words_x", "d2w")
+        w2s = place_scales(d2s, nc.sync, "w2s")
+        w2 = work.tile([P, H], I32, name="w2", align_bytes=64)
+        deal(w2[:], d2w[:].bitcast(I32), slice(0, PACK))
+
+        hs = work.tile([P, PACK, S], F32, name="hs")
+        for t in range(PACK):
+            nc.vector.tensor_scalar(hs[:, t, :], layer1[t][0][:], gs_sb[:, t : t + 1], 0.5, ALU.mult, ALU.mult)
+
+        zw = work.tile([P, S], U32, name="zw", align_bytes=64)
+        zs = work.tile([P, S], U8, name="zs", align_bytes=64)
+        banks2 = [psum.tile([P, S], F32, name="bank2_%d" % t) for t in range(PACK)]
+        units = [(lo, hi, t) for lo, hi in HALVES for t in range(PACK)]
+        logs = work.tile([P, len(units), 2, S // 2], F32, name="logs")
+        diff = work.tile([P, len(units), S // 2], F32, name="diff")
+        z_rows = [work.tile([P, PACK, S // 2], BF16, name="z_rows%d" % lo) for lo, hi in HALVES]
+        for u, (lo, hi, t) in enumerate(units):
+            nc.scalar.activation(logs[:, u, :, :], ea[:, t, :, lo:hi], ACT.Ln, bias=0.25)
+
+        def weigh(u):
+            lo, hi, t = units[u]
+            nc.vector.scalar_tensor_tensor(
+                z_rows[u // PACK][:, t, :], diff[:, u, :], gs_sb[:, t : t + 1], hs[:, t, lo:hi], ALU.mult, ALU.add,
+            )
+
+        for u in range(len(units)):
+            nc.vector.tensor_tensor(diff[:, u, :], logs[:, u, 0, :], logs[:, u, 1, :], ALU.subtract)
+            if u > 0:
+                weigh(u - 1)
+        weigh(len(units) - 1)
+        for c, (lo, hi) in enumerate(HALVES):
+            z_side = work.tile([P, hi - lo, PACK], BF16, name="z_side%d" % lo, align_bytes=64)
+            copy = nc.vector.tensor_copy if hi == S else nc.scalar.copy
+            copy(
+                z_side[:].rearrange("p (c i) t -> p c t i", i=4),
+                z_rows[c][:].rearrange("p t (c i) -> p c t i", i=4),
+            )
+            nc.vector.quantize_mx(
+                out=zw[:, lo:hi].bitcast(FP8X4), scales=zs[:, lo:hi],
+                in_=z_side[:].rearrange("p n t -> p (n t)"),
+            )
+            multiply(banks2[0], slice(lo, hi), 0, w2, w2s, zw, zs)
+        for t in range(1, PACK):
+            multiply(banks2[t], slice(0, S), t, w2, w2s, zw, zs)
+
+        layer2 = [leave_bank(banks2[t], t, neg34, "g") for t in range(PACK)]
+        ow = work.tile([P, S], U32, name="ow", align_bytes=64)
+        osc = work.tile([P, S], U8, name="osc", align_bytes=64)
+        out_rows = out_0.rearrange("(p t) j -> p t j", t=PACK)
+        out_words = out_1[0].rearrange("p n t -> p (n t)").bitcast(I32)
+        out_scales = out_2[0].bitcast(I32)
+        for lo, hi in OUT_PIECES:
+            n = hi - lo
+            eb = work.tile([P, PACK, 2, n], F32, name="eb%d" % lo)
+            for t in range(PACK):
+                g, bias = layer2[t]
+                fetch_exp(eb[:, t, 0, :], g, n3_sb, lo, hi, tau3_sb[:, t : t + 1], bias[:, 0:1])
+                fetch_exp(eb[:, t, 1, :], g, n4_sb, lo, hi, tau4_sb[:, t : t + 1], bias[:, 1:2])
+            gap = work.tile([P, PACK, n], F32, name="gap%d" % lo)
+            y = work.tile([P, PACK, n], F32, name="y%d" % lo)
+            for ts in ([slice(0, 3), slice(3, 4)] if hi == S else [slice(0, PACK)]):
+                nc.vector.tensor_tensor(gap[:, ts, :], eb[:, ts, 0, :], eb[:, ts, 1, :], ALU.subtract)
+                nc.vector.tensor_scalar(y[:, ts, :], gap[:, ts, :], 3.0, None, ALU.mult)
+                nc.sync.dma_start(out_rows[:, ts, lo:hi], y[:, ts, :])
+            y_side = work.tile([P, n, PACK], BF16, name="y_side%d" % lo, align_bytes=64)
+            nc.vector.tensor_copy(
+                y_side[:].rearrange("p (c i) t -> p c t i", i=4),
+                y[:].rearrange("p t (c i) -> p c t i", i=4),
+            )
+            nc.vector.quantize_mx(
+                out=ow[:, lo:hi].bitcast(FP8X4), scales=osc[:, lo:hi],
+                in_=y_side[:].rearrange("p n t -> p (n t)"),
+            )
+            nc.sync.dma_start(out_words[:, lo:hi], ow[:, lo:hi].bitcast(I32))
+        for r in range(4):
+            queue = nc.sync if r % 2 == 0 else nc.scalar
+            queue.dma_start(out_scales[r:16:4, :], osc[r:P:32, :].bitcast(I32))

@@ -17,7 +17,8 @@ PACK = 4
 K, T, S, G, H = 512, 1024, 512, 2048, 512
 FLOPS = 2 * 2 * K * H * S
 
-OUT_PIECES = [(0, 256), (256, 384), (384, 512)]
+TAIL_SPLIT = 160
+SPLIT = 160
 HALVES = [(0, 256), (256, 512)]
 
 
@@ -45,6 +46,8 @@ def tile_picked_codeeosetw_none_po_kernel(
         xs_tab = keep.tile([P, T], U8, name="xs_tab")
         nc.vector.memset(ds_tab[:].bitcast(I32), 0)
         nc.vector.memset(xs_tab[:].bitcast(I32), 0)
+        win1 = [keep.tile([P, S], F32, name="win1_%d" % t) for t in range(PACK)]
+        win2 = [keep.tile([P, S], F32, name="win2_%d" % t) for t in range(PACK)]
         k1_sb = load_list(k1, "k1_sb")
         ds_rows = d_scales[0].bitcast(I32)
         for e in range(2):
@@ -60,8 +63,7 @@ def tile_picked_codeeosetw_none_po_kernel(
         tau2_sb = load_rows(tau2, "tau2_sb")
         xs_rows = x_scales[0].bitcast(I32)
         for r in range(4):
-            queue = nc.scalar if r < 2 else nc.gpsimd
-            queue.dma_start(xs_tab[r:P:32, :].bitcast(I32), xs_rows[r:16:4, :])
+            nc.scalar.dma_start(xs_tab[r:P:32, :].bitcast(I32), xs_rows[r:16:4, :])
         gs_sb = load_rows(gs, "gs_sb")
         tau3_sb = load_rows(tau3, "tau3_sb")
         tau4_sb = load_rows(tau4, "tau4_sb")
@@ -94,20 +96,26 @@ def tile_picked_codeeosetw_none_po_kernel(
                 queue.dma_start(dealt[2 + e : P : 32, :].bitcast(I32), dealt[16 + e : P : 32, :].bitcast(I32))
             return dealt
 
-        def multiply(bank, cols, t, w, ws, a, a_s):
+        def multiply(tag, cols, t, w, ws, a, a_s):
+            bank = psum.tile([P, cols.stop - cols.start], F32, name="bank", tag=tag)
             m = slice(t * P, (t + 1) * P)
             nc.tensor.matmul_mx(
-                out=bank[:, cols], lhsT=w[:, m].bitcast(FP8X4), lhsT_scale=ws[:, m],
+                out=bank[:], lhsT=w[t].bitcast(FP8X4), lhsT_scale=ws[:, m],
                 rhs=a[:, cols].bitcast(FP8X4), rhs_scale=a_s[:, cols], start=True, stop=True,
             )
+            return bank, cols
 
-        def leave_bank(bank, t, neg, name):
-            rows = work.tile([P, S], F32, name="%s%d" % (name, t))
-            top = work.tile([P, 1], F32, name="%s_top%d" % (name, t))
-            nc.vector.tensor_scalar(rows[:], bank[:], 0.0625, None, ALU.mult, ALU.max, accum_out=top[:])
-            bias = work.tile([P, 2], F32, name="%s_bias%d" % (name, t))
-            nc.vector.tensor_scalar(bias[:], neg[:, t, :], top[:], None, ALU.mult)
-            return rows, bias
+        def leave_banks(parts, window, neg, name):
+            tops = []
+            for bank, cols in parts:
+                top = work.tile([P, 1], F32, name="%s_top%d" % (name, cols.start))
+                nc.vector.tensor_scalar(window[:, cols], bank[:], 0.0625, None, ALU.mult, ALU.max, accum_out=top[:])
+                tops.append(top)
+            bias = work.tile([P, 2], F32, name=name + "_bias")
+            nc.vector.scalar_tensor_tensor(
+                bias[:], tops[0][:].to_broadcast([P, 2]), tops[-1][:], neg, ALU.max, ALU.mult,
+            )
+            return bias
 
         def fetch_exp(dst, rows, places, lo, hi, rate, bias):
             nc.scalar.activation(
@@ -116,45 +124,59 @@ def tile_picked_codeeosetw_none_po_kernel(
 
         dw_words = dw_tab[:].bitcast(U32)
         d1s = pick(ds_tab[:], k1_sb, U8, "scales_d", "d1s")
-        xw = pick(xw_tab[:].bitcast(U32), offs_sb, U32, "words_x", "xw")
         w1s = place_scales(d1s, nc.sync, "w1s")
+        xw = pick(xw_tab[:].bitcast(U32), offs_sb, U32, "words_x", "xw")
         d1w = pick(dw_words, k1_sb, U32, "words_d", "d1w")
         xs = pick(xs_tab[:], offs_sb, U8, "scales_x", "xs")
-        w1 = work.tile([P, H], I32, name="w1", align_bytes=64)
-        deal(w1[:], d1w[:].bitcast(I32), slice(0, 1))
-        deal(w1[:], d1w[:].bitcast(I32), slice(1, PACK))
+        d1w_by_tile = d1w[:].bitcast(I32).rearrange("p (m t) -> p m t", t=PACK)
+        w1_first = work.tile([P, P], I32, name="w1_first", align_bytes=64)
+        nc.vector.tensor_copy(w1_first[:], d1w_by_tile[:, :, 0])
+        w1_rest = work.tile([P, PACK - 1, P], I32, name="w1_rest", align_bytes=64)
+        nc.vector.tensor_copy(w1_rest[:].rearrange("p t m -> p m t"), d1w_by_tile[:, :, 1:])
+        w1 = [w1_first[:]] + [w1_rest[:, t, :] for t in range(PACK - 1)]
 
-        banks1 = [psum.tile([P, S], F32, name="bank1_%d" % t) for t in range(PACK)]
-        for t in range(PACK):
-            multiply(banks1[t], slice(0, S), t, w1, w1s, xw, xs)
-        layer1 = [leave_bank(banks1[t], t, neg12, "h") for t in range(PACK)]
+        parts1 = [[multiply("b0%d" % lo, slice(lo, hi), 0, w1, w1s, xw, xs) for lo, hi in HALVES]]
+        for t in range(1, PACK):
+            parts1.append([multiply("b%d" % t, slice(0, S), t, w1, w1s, xw, xs)])
+        bias1 = [leave_banks(parts1[t], win1[t], neg12[:, t, :], "h%d" % t) for t in range(PACK)]
 
         ea = work.tile([P, PACK, 2, S], F32, name="ea")
         for t in range(PACK):
-            h, bias = layer1[t]
             for lo, hi in HALVES:
-                fetch_exp(ea[:, t, 0, lo:hi], h, n1_sb, lo, hi, tau_sb[:, t : t + 1], bias[:, 0:1])
-                fetch_exp(ea[:, t, 1, lo:hi], h, n2_sb, lo, hi, tau2_sb[:, t : t + 1], bias[:, 1:2])
+                fetch_exp(ea[:, t, 1, lo:hi], win1[t], n2_sb, lo, hi, tau2_sb[:, t : t + 1], bias1[t][:, 1:2])
+            for lo, hi in HALVES:
+                fetch_exp(ea[:, t, 0, lo:hi], win1[t], n1_sb, lo, hi, tau_sb[:, t : t + 1], bias1[t][:, 0:1])
 
         d2s = pick(ds_tab[:], k2_sb, U8, "scales_x", "d2s")
         d2w = pick(dw_words, k2_sb, U32, "words_x", "d2w")
         w2s = place_scales(d2s, nc.sync, "w2s")
-        w2 = work.tile([P, H], I32, name="w2", align_bytes=64)
-        deal(w2[:], d2w[:].bitcast(I32), slice(0, PACK))
+        w2_all = work.tile([P, H], I32, name="w2_all", align_bytes=64)
+        deal(w2_all[:], d2w[:].bitcast(I32), slice(0, PACK))
+        w2 = [w2_all[:, t * P : (t + 1) * P] for t in range(PACK)]
 
         hs = work.tile([P, PACK, S], F32, name="hs")
         for t in range(PACK):
-            nc.vector.tensor_scalar(hs[:, t, :], layer1[t][0][:], gs_sb[:, t : t + 1], 0.5, ALU.mult, ALU.mult)
+            nc.vector.tensor_scalar(hs[:, t, :], win1[t][:], gs_sb[:, t : t + 1], 0.5, ALU.mult, ALU.mult)
 
         zw = work.tile([P, S], U32, name="zw", align_bytes=64)
         zs = work.tile([P, S], U8, name="zs", align_bytes=64)
-        banks2 = [psum.tile([P, S], F32, name="bank2_%d" % t) for t in range(PACK)]
+        parts2 = [[]]
+        below = work.tile([P, S], F32, name="below")
+        nc.vector.tensor_scalar(below[:], ea[:, 0, 1, :], 0.25, None, ALU.add)
+        inverse = work.tile([P, S], F32, name="inverse", tag="logs")
+        nc.vector.reciprocal(inverse[:], below[:])
+        ratio = work.tile([P, S], F32, name="ratio")
+        nc.vector.scalar_tensor_tensor(ratio[:], ea[:, 0, 0, :], 0.25, inverse[:], ALU.add, ALU.mult)
+
         units = [(lo, hi, t) for lo, hi in HALVES for t in range(PACK)]
-        logs = work.tile([P, len(units), 2, S // 2], F32, name="logs")
+        logs = work.tile([P, len(units), 2, S // 2], F32, name="logs", tag="logs")
         diff = work.tile([P, len(units), S // 2], F32, name="diff")
         z_rows = [work.tile([P, PACK, S // 2], BF16, name="z_rows%d" % lo) for lo, hi in HALVES]
         for u, (lo, hi, t) in enumerate(units):
-            nc.scalar.activation(logs[:, u, :, :], ea[:, t, :, lo:hi], ACT.Ln, bias=0.25)
+            if t == 0:
+                nc.scalar.activation(diff[:, u, :], ratio[:, lo:hi], ACT.Ln)
+            else:
+                nc.scalar.activation(logs[:, u, :, :], ea[:, t, :, lo:hi], ACT.Ln, bias=0.25)
 
         def weigh(u):
             lo, hi, t = units[u]
@@ -162,55 +184,65 @@ def tile_picked_codeeosetw_none_po_kernel(
                 z_rows[u // PACK][:, t, :], diff[:, u, :], gs_sb[:, t : t + 1], hs[:, t, lo:hi], ALU.mult, ALU.add,
             )
 
-        for u in range(len(units)):
-            nc.vector.tensor_tensor(diff[:, u, :], logs[:, u, 0, :], logs[:, u, 1, :], ALU.subtract)
+        for u, (lo, hi, t) in enumerate(units):
+            if t > 0:
+                nc.vector.tensor_tensor(diff[:, u, :], logs[:, u, 0, :], logs[:, u, 1, :], ALU.subtract)
             if u > 0:
                 weigh(u - 1)
         weigh(len(units) - 1)
         for c, (lo, hi) in enumerate(HALVES):
             z_side = work.tile([P, hi - lo, PACK], BF16, name="z_side%d" % lo, align_bytes=64)
-            copy = nc.vector.tensor_copy if hi == S else nc.scalar.copy
-            copy(
-                z_side[:].rearrange("p (c i) t -> p c t i", i=4),
-                z_rows[c][:].rearrange("p t (c i) -> p c t i", i=4),
-            )
+            n = hi - lo
+            shares = [(nc.scalar.copy, 0, n)] if hi < S else [(nc.vector.tensor_copy, 0, SPLIT), (nc.scalar.copy, SPLIT, n)]
+            for copy, a, b in shares:
+                copy(
+                    z_side[:, a:b, :].rearrange("p (c i) t -> p c t i", i=4),
+                    z_rows[c][:, :, a:b].rearrange("p t (c i) -> p c t i", i=4),
+                )
             nc.vector.quantize_mx(
                 out=zw[:, lo:hi].bitcast(FP8X4), scales=zs[:, lo:hi],
                 in_=z_side[:].rearrange("p n t -> p (n t)"),
             )
-            multiply(banks2[0], slice(lo, hi), 0, w2, w2s, zw, zs)
+            parts2[0].append(multiply("b0%d" % lo, slice(lo, hi), 0, w2, w2s, zw, zs))
         for t in range(1, PACK):
-            multiply(banks2[t], slice(0, S), t, w2, w2s, zw, zs)
+            parts2.append([multiply("b%d" % t, slice(0, S), t, w2, w2s, zw, zs)])
 
-        layer2 = [leave_bank(banks2[t], t, neg34, "g") for t in range(PACK)]
+        bias2 = [leave_banks(parts2[t], win2[t], neg34[:, t, :], "g%d" % t) for t in range(PACK)]
         ow = work.tile([P, S], U32, name="ow", align_bytes=64)
         osc = work.tile([P, S], U8, name="osc", align_bytes=64)
         out_rows = out_0.rearrange("(p t) j -> p t j", t=PACK)
         out_words = out_1[0].rearrange("p n t -> p (n t)").bitcast(I32)
         out_scales = out_2[0].bitcast(I32)
-        for lo, hi in OUT_PIECES:
+        for lo, hi in HALVES:
             n = hi - lo
             eb = work.tile([P, PACK, 2, n], F32, name="eb%d" % lo)
-            for t in range(PACK):
-                g, bias = layer2[t]
-                fetch_exp(eb[:, t, 0, :], g, n3_sb, lo, hi, tau3_sb[:, t : t + 1], bias[:, 0:1])
-                fetch_exp(eb[:, t, 1, :], g, n4_sb, lo, hi, tau4_sb[:, t : t + 1], bias[:, 1:2])
             gap = work.tile([P, PACK, n], F32, name="gap%d" % lo)
             y = work.tile([P, PACK, n], F32, name="y%d" % lo)
-            for ts in ([slice(0, 3), slice(3, 4)] if hi == S else [slice(0, PACK)]):
+            y_side = work.tile([P, n, PACK], BF16, name="y_side%d" % lo, align_bytes=64)
+            for t in range(PACK):
+                fetch_exp(eb[:, t, 0, :], win2[t], n3_sb, lo, hi, tau3_sb[:, t : t + 1], bias2[t][:, 0:1])
+                fetch_exp(eb[:, t, 1, :], win2[t], n4_sb, lo, hi, tau4_sb[:, t : t + 1], bias2[t][:, 1:2])
+            for ts in ([slice(0, 2), slice(2, 3), slice(3, 4)] if hi == S else [slice(0, 2), slice(2, PACK)]):
                 nc.vector.tensor_tensor(gap[:, ts, :], eb[:, ts, 0, :], eb[:, ts, 1, :], ALU.subtract)
+                if ts.stop == PACK:
+                    cut = TAIL_SPLIT if hi == S else n
+                    nc.vector.tensor_scalar(
+                        y_side[:, :cut, :].rearrange("p (c i) t -> p c t i", i=4),
+                        gap[:, :, :cut].rearrange("p t (c i) -> p c t i", i=4), 3.0, None, ALU.mult,
+                    )
+                    if cut < n:
+                        nc.scalar.activation(
+                            y_side[:, cut:, :].rearrange("p (c i) t -> p c t i", i=4),
+                            gap[:, :, cut:].rearrange("p t (c i) -> p c t i", i=4), ACT.Copy, scale=3.0,
+                        )
                 nc.vector.tensor_scalar(y[:, ts, :], gap[:, ts, :], 3.0, None, ALU.mult)
                 nc.sync.dma_start(out_rows[:, ts, lo:hi], y[:, ts, :])
-            y_side = work.tile([P, n, PACK], BF16, name="y_side%d" % lo, align_bytes=64)
-            nc.vector.tensor_copy(
-                y_side[:].rearrange("p (c i) t -> p c t i", i=4),
-                y[:].rearrange("p t (c i) -> p c t i", i=4),
-            )
             nc.vector.quantize_mx(
                 out=ow[:, lo:hi].bitcast(FP8X4), scales=osc[:, lo:hi],
                 in_=y_side[:].rearrange("p n t -> p (n t)"),
             )
-            nc.sync.dma_start(out_words[:, lo:hi], ow[:, lo:hi].bitcast(I32))
+            queue = nc.scalar if hi == S else nc.sync
+            queue.dma_start(out_words[:, lo:hi], ow[:, lo:hi].bitcast(I32))
         for r in range(4):
             queue = nc.sync if r % 2 == 0 else nc.scalar
             queue.dma_start(out_scales[r:16:4, :], osc[r:P:32, :].bitcast(I32))

@@ -18,7 +18,6 @@ K, T, S, G, H = 512, 1024, 512, 2048, 512
 FLOPS = 2 * 2 * K * H * S
 
 TAIL_SPLIT = 160
-SPLIT = 160
 HALVES = [(0, 256), (256, 512)]
 
 
@@ -46,8 +45,10 @@ def tile_picked_codeeosetw_none_po_kernel(
         xs_tab = keep.tile([P, T], U8, name="xs_tab")
         nc.vector.memset(ds_tab[:].bitcast(I32), 0)
         nc.vector.memset(xs_tab[:].bitcast(I32), 0)
-        win1 = [keep.tile([P, S], F32, name="win1_%d" % t) for t in range(PACK)]
-        win2 = [keep.tile([P, S], F32, name="win2_%d" % t) for t in range(PACK)]
+        win1 = [keep.tile([P, 2 * S if t > 0 else S], F32, name="win1_%d" % t) for t in range(PACK)]
+        win2 = [keep.tile([P, 2 * S if t < 2 else S], F32, name="win2_%d" % t) for t in range(PACK)]
+        hs = [win1[1][:, S:], win1[2][:, S:], win1[3][:, S:], win2[0][:, S:]]
+        ratio = win2[1][:, S:]
         k1_sb = load_list(k1, "k1_sb")
         ds_rows = d_scales[0].bitcast(I32)
         for e in range(2):
@@ -122,6 +123,9 @@ def tile_picked_codeeosetw_none_po_kernel(
                 dst, rows[:].indirect(places[:, lo // 16 : hi // 16]), ACT.Exp, bias=bias, scale=rate,
             )
 
+        def halve(t):
+            nc.vector.tensor_scalar(hs[t], win1[t][:, :S], gs_sb[:, t : t + 1], 0.5, ALU.mult, ALU.mult)
+
         dw_words = dw_tab[:].bitcast(U32)
         d1s = pick(ds_tab[:], k1_sb, U8, "scales_d", "d1s")
         w1s = place_scales(d1s, nc.sync, "w1s")
@@ -138,14 +142,16 @@ def tile_picked_codeeosetw_none_po_kernel(
         parts1 = [[multiply("b0%d" % lo, slice(lo, hi), 0, w1, w1s, xw, xs) for lo, hi in HALVES]]
         for t in range(1, PACK):
             parts1.append([multiply("b%d" % t, slice(0, S), t, w1, w1s, xw, xs)])
-        bias1 = [leave_banks(parts1[t], win1[t], neg12[:, t, :], "h%d" % t) for t in range(PACK)]
-
         ea = work.tile([P, PACK, 2, S], F32, name="ea")
         for t in range(PACK):
-            for lo, hi in HALVES:
-                fetch_exp(ea[:, t, 1, lo:hi], win1[t], n2_sb, lo, hi, tau2_sb[:, t : t + 1], bias1[t][:, 1:2])
-            for lo, hi in HALVES:
-                fetch_exp(ea[:, t, 0, lo:hi], win1[t], n1_sb, lo, hi, tau_sb[:, t : t + 1], bias1[t][:, 0:1])
+            bias = leave_banks(parts1[t], win1[t], neg12[:, t, :], "h%d" % t)
+            if t > 0:
+                halve(t - 1)
+            cuts = HALVES if t == 0 else [(0, S)]
+            for lo, hi in cuts:
+                fetch_exp(ea[:, t, 1, lo:hi], win1[t], n2_sb, lo, hi, tau2_sb[:, t : t + 1], bias[:, 1:2])
+            for lo, hi in cuts:
+                fetch_exp(ea[:, t, 0, lo:hi], win1[t], n1_sb, lo, hi, tau_sb[:, t : t + 1], bias[:, 0:1])
 
         d2s = pick(ds_tab[:], k2_sb, U8, "scales_x", "d2s")
         d2w = pick(dw_words, k2_sb, U32, "words_x", "d2w")
@@ -154,9 +160,7 @@ def tile_picked_codeeosetw_none_po_kernel(
         deal(w2_all[:], d2w[:].bitcast(I32), slice(0, PACK))
         w2 = [w2_all[:, t * P : (t + 1) * P] for t in range(PACK)]
 
-        hs = work.tile([P, PACK, S], F32, name="hs")
-        for t in range(PACK):
-            nc.vector.tensor_scalar(hs[:, t, :], win1[t][:], gs_sb[:, t : t + 1], 0.5, ALU.mult, ALU.mult)
+        halve(PACK - 1)
 
         zw = work.tile([P, S], U32, name="zw", align_bytes=64)
         zs = work.tile([P, S], U8, name="zs", align_bytes=64)
@@ -165,10 +169,9 @@ def tile_picked_codeeosetw_none_po_kernel(
         nc.vector.tensor_scalar(below[:], ea[:, 0, 1, :], 0.25, None, ALU.add)
         inverse = work.tile([P, S], F32, name="inverse", tag="logs")
         nc.vector.reciprocal(inverse[:], below[:])
-        ratio = work.tile([P, S], F32, name="ratio")
-        nc.vector.scalar_tensor_tensor(ratio[:], ea[:, 0, 0, :], 0.25, inverse[:], ALU.add, ALU.mult)
+        nc.vector.scalar_tensor_tensor(ratio, ea[:, 0, 0, :], 0.25, inverse[:], ALU.add, ALU.mult)
 
-        units = [(lo, hi, t) for lo, hi in HALVES for t in range(PACK)]
+        units = [HALVES[0] + (t,) for t in (0, 1, 2, 3)] + [HALVES[1] + (t,) for t in (1, 2, 3, 0)]
         logs = work.tile([P, len(units), 2, S // 2], F32, name="logs", tag="logs")
         diff = work.tile([P, len(units), S // 2], F32, name="diff")
         z_rows = [work.tile([P, PACK, S // 2], BF16, name="z_rows%d" % lo) for lo, hi in HALVES]
@@ -181,7 +184,7 @@ def tile_picked_codeeosetw_none_po_kernel(
         def weigh(u):
             lo, hi, t = units[u]
             nc.vector.scalar_tensor_tensor(
-                z_rows[u // PACK][:, t, :], diff[:, u, :], gs_sb[:, t : t + 1], hs[:, t, lo:hi], ALU.mult, ALU.add,
+                z_rows[u // PACK][:, t, :], diff[:, u, :], gs_sb[:, t : t + 1], hs[t][:, lo:hi], ALU.mult, ALU.add,
             )
 
         for u, (lo, hi, t) in enumerate(units):
@@ -190,18 +193,16 @@ def tile_picked_codeeosetw_none_po_kernel(
             if u > 0:
                 weigh(u - 1)
         weigh(len(units) - 1)
+        z_side = [work.tile([P, S // 2, PACK], BF16, name="z_side%d" % lo, align_bytes=64) for lo, hi in HALVES]
+        for c, copy in enumerate([nc.scalar.copy, nc.vector.tensor_copy]):
+            copy(
+                z_side[c][:].rearrange("p (c i) t -> p c t i", i=4),
+                z_rows[c][:].rearrange("p t (c i) -> p c t i", i=4),
+            )
         for c, (lo, hi) in enumerate(HALVES):
-            z_side = work.tile([P, hi - lo, PACK], BF16, name="z_side%d" % lo, align_bytes=64)
-            n = hi - lo
-            shares = [(nc.scalar.copy, 0, n)] if hi < S else [(nc.vector.tensor_copy, 0, SPLIT), (nc.scalar.copy, SPLIT, n)]
-            for copy, a, b in shares:
-                copy(
-                    z_side[:, a:b, :].rearrange("p (c i) t -> p c t i", i=4),
-                    z_rows[c][:, :, a:b].rearrange("p t (c i) -> p c t i", i=4),
-                )
             nc.vector.quantize_mx(
                 out=zw[:, lo:hi].bitcast(FP8X4), scales=zs[:, lo:hi],
-                in_=z_side[:].rearrange("p n t -> p (n t)"),
+                in_=z_side[c][:].rearrange("p n t -> p (n t)"),
             )
             parts2[0].append(multiply("b0%d" % lo, slice(lo, hi), 0, w2, w2s, zw, zs))
         for t in range(1, PACK):
@@ -213,33 +214,51 @@ def tile_picked_codeeosetw_none_po_kernel(
         out_rows = out_0.rearrange("(p t) j -> p t j", t=PACK)
         out_words = out_1[0].rearrange("p n t -> p (n t)").bitcast(I32)
         out_scales = out_2[0].bitcast(I32)
+        eb = work.tile([P, PACK, 2, S], F32, name="eb")
+        gap = work.tile([P, PACK, S], F32, name="gap")
+        y = work.tile([P, PACK, S], F32, name="y")
+
+        def fetch_pair(t, lo, hi):
+            fetch_exp(eb[:, t, 0, lo:hi], win2[t], n3_sb, lo, hi, tau3_sb[:, t : t + 1], bias2[t][:, 0:1])
+            fetch_exp(eb[:, t, 1, lo:hi], win2[t], n4_sb, lo, hi, tau4_sb[:, t : t + 1], bias2[t][:, 1:2])
+
+        def subtract(t, lo, hi):
+            nc.vector.tensor_tensor(gap[:, t, lo:hi], eb[:, t, 0, lo:hi], eb[:, t, 1, lo:hi], ALU.subtract)
+
+        def store_rows(ts, lo, hi):
+            nc.vector.tensor_scalar(y[:, ts, lo:hi], gap[:, ts, lo:hi], 3.0, None, ALU.mult)
+            nc.sync.dma_start(out_rows[:, ts, lo:hi], y[:, ts, lo:hi])
+
+        def side_views(side, lo, a, b):
+            return (
+                side[:, a:b, :].rearrange("p (c i) t -> p c t i", i=4),
+                gap[:, :, lo + a : lo + b].rearrange("p t (c i) -> p c t i", i=4),
+            )
+
+        mid = S // 2
+        for t in (0, 1):
+            fetch_pair(t, 0, S)
         for lo, hi in HALVES:
-            n = hi - lo
-            eb = work.tile([P, PACK, 2, n], F32, name="eb%d" % lo)
-            gap = work.tile([P, PACK, n], F32, name="gap%d" % lo)
-            y = work.tile([P, PACK, n], F32, name="y%d" % lo)
-            y_side = work.tile([P, n, PACK], BF16, name="y_side%d" % lo, align_bytes=64)
-            for t in range(PACK):
-                fetch_exp(eb[:, t, 0, :], win2[t], n3_sb, lo, hi, tau3_sb[:, t : t + 1], bias2[t][:, 0:1])
-                fetch_exp(eb[:, t, 1, :], win2[t], n4_sb, lo, hi, tau4_sb[:, t : t + 1], bias2[t][:, 1:2])
-            for ts in ([slice(0, 2), slice(2, 3), slice(3, 4)] if hi == S else [slice(0, 2), slice(2, PACK)]):
-                nc.vector.tensor_tensor(gap[:, ts, :], eb[:, ts, 0, :], eb[:, ts, 1, :], ALU.subtract)
-                if ts.stop == PACK:
-                    cut = TAIL_SPLIT if hi == S else n
-                    nc.vector.tensor_scalar(
-                        y_side[:, :cut, :].rearrange("p (c i) t -> p c t i", i=4),
-                        gap[:, :, :cut].rearrange("p t (c i) -> p c t i", i=4), 3.0, None, ALU.mult,
-                    )
-                    if cut < n:
-                        nc.scalar.activation(
-                            y_side[:, cut:, :].rearrange("p (c i) t -> p c t i", i=4),
-                            gap[:, :, cut:].rearrange("p t (c i) -> p c t i", i=4), ACT.Copy, scale=3.0,
-                        )
-                nc.vector.tensor_scalar(y[:, ts, :], gap[:, ts, :], 3.0, None, ALU.mult)
-                nc.sync.dma_start(out_rows[:, ts, lo:hi], y[:, ts, :])
+            for t in (2, 3):
+                fetch_pair(t, lo, hi)
+
+        for t in (0, 1):
+            subtract(t, 0, S)
+            store_rows(slice(t, t + 1), 0, S)
+        for lo, hi in HALVES:
+            subtract(2, lo, hi)
+            if hi == S:
+                store_rows(slice(2, 3), lo, hi)
+            subtract(3, lo, hi)
+            side = work.tile([P, hi - lo, PACK], BF16, name="y_side%d" % lo, align_bytes=64)
+            cut = TAIL_SPLIT if hi == S else mid
+            nc.vector.tensor_scalar(*side_views(side, lo, 0, cut), 3.0, None, ALU.mult)
+            if cut < mid:
+                nc.scalar.activation(*side_views(side, lo, cut, mid), ACT.Copy, scale=3.0)
+            store_rows(slice(3, 4) if hi == S else slice(2, 4), lo, hi)
             nc.vector.quantize_mx(
                 out=ow[:, lo:hi].bitcast(FP8X4), scales=osc[:, lo:hi],
-                in_=y_side[:].rearrange("p n t -> p (n t)"),
+                in_=side[:].rearrange("p n t -> p (n t)"),
             )
             queue = nc.scalar if hi == S else nc.sync
             queue.dma_start(out_words[:, lo:hi], ow[:, lo:hi].bitcast(I32))

@@ -17,7 +17,6 @@ PACK = 4
 K, T, S, G, H = 512, 1024, 512, 2048, 512
 FLOPS = 2 * 2 * K * H * S
 
-TAIL_SPLIT = 160
 HALVES = [(0, 256), (256, 512)]
 
 
@@ -46,9 +45,8 @@ def tile_picked_codeeosetw_none_po_kernel(
         nc.vector.memset(ds_tab[:].bitcast(I32), 0)
         nc.vector.memset(xs_tab[:].bitcast(I32), 0)
         win1 = [keep.tile([P, 2 * S if t > 0 else S], F32, name="win1_%d" % t) for t in range(PACK)]
-        win2 = [keep.tile([P, 2 * S if t < 2 else S], F32, name="win2_%d" % t) for t in range(PACK)]
+        win2 = [keep.tile([P, 2 * S if t == 0 else S], F32, name="win2_%d" % t) for t in range(PACK)]
         hs = [win1[1][:, S:], win1[2][:, S:], win1[3][:, S:], win2[0][:, S:]]
-        ratio = win2[1][:, S:]
         k1_sb = load_list(k1, "k1_sb")
         ds_rows = d_scales[0].bitcast(I32)
         for e in range(2):
@@ -162,19 +160,19 @@ def tile_picked_codeeosetw_none_po_kernel(
 
         halve(PACK - 1)
 
-        zw = work.tile([P, S], U32, name="zw", align_bytes=64)
         zs = work.tile([P, S], U8, name="zs", align_bytes=64)
         parts2 = [[]]
         below = work.tile([P, S], F32, name="below")
         nc.vector.tensor_scalar(below[:], ea[:, 0, 1, :], 0.25, None, ALU.add)
         inverse = work.tile([P, S], F32, name="inverse", tag="logs")
         nc.vector.reciprocal(inverse[:], below[:])
-        nc.vector.scalar_tensor_tensor(ratio, ea[:, 0, 0, :], 0.25, inverse[:], ALU.add, ALU.mult)
+        ratio = work.tile([P, S], F32, name="ratio")
+        nc.vector.scalar_tensor_tensor(ratio[:], ea[:, 0, 0, :], 0.25, inverse[:], ALU.add, ALU.mult)
 
         units = [HALVES[0] + (t,) for t in (0, 1, 2, 3)] + [HALVES[1] + (t,) for t in (1, 2, 3, 0)]
         logs = work.tile([P, len(units), 2, S // 2], F32, name="logs", tag="logs")
         diff = work.tile([P, len(units), S // 2], F32, name="diff")
-        z_rows = [work.tile([P, PACK, S // 2], BF16, name="z_rows%d" % lo) for lo, hi in HALVES]
+        z_rows = [work.tile([P, PACK, S // 2], BF16, name="z_rows%d" % lo, tag="z_rows%d" % lo, align_bytes=64) for lo, hi in HALVES]
         for u, (lo, hi, t) in enumerate(units):
             if t == 0:
                 nc.scalar.activation(diff[:, u, :], ratio[:, lo:hi], ACT.Ln)
@@ -187,11 +185,12 @@ def tile_picked_codeeosetw_none_po_kernel(
                 z_rows[u // PACK][:, t, :], diff[:, u, :], gs_sb[:, t : t + 1], hs[t][:, lo:hi], ALU.mult, ALU.add,
             )
 
-        for u, (lo, hi, t) in enumerate(units):
-            if t > 0:
-                nc.vector.tensor_tensor(diff[:, u, :], logs[:, u, 0, :], logs[:, u, 1, :], ALU.subtract)
-            if u > 0:
+        weigh(0)
+        for u in range(1, len(units) - 1):
+            nc.vector.tensor_tensor(diff[:, u, :], logs[:, u, 0, :], logs[:, u, 1, :], ALU.subtract)
+            if u > 1:
                 weigh(u - 1)
+        weigh(len(units) - 2)
         weigh(len(units) - 1)
         z_side = [work.tile([P, S // 2, PACK], BF16, name="z_side%d" % lo, align_bytes=64) for lo, hi in HALVES]
         for c, copy in enumerate([nc.scalar.copy, nc.vector.tensor_copy]):
@@ -199,6 +198,7 @@ def tile_picked_codeeosetw_none_po_kernel(
                 z_side[c][:].rearrange("p (c i) t -> p c t i", i=4),
                 z_rows[c][:].rearrange("p t (c i) -> p c t i", i=4),
             )
+        zw = work.tile([P, S], U32, name="zw", tag="z_rows256", align_bytes=64)
         for c, (lo, hi) in enumerate(HALVES):
             nc.vector.quantize_mx(
                 out=zw[:, lo:hi].bitcast(FP8X4), scales=zs[:, lo:hi],
@@ -218,50 +218,54 @@ def tile_picked_codeeosetw_none_po_kernel(
         gap = work.tile([P, PACK, S], F32, name="gap")
         y = work.tile([P, PACK, S], F32, name="y")
 
-        def fetch_pair(t, lo, hi):
-            fetch_exp(eb[:, t, 0, lo:hi], win2[t], n3_sb, lo, hi, tau3_sb[:, t : t + 1], bias2[t][:, 0:1])
-            fetch_exp(eb[:, t, 1, lo:hi], win2[t], n4_sb, lo, hi, tau4_sb[:, t : t + 1], bias2[t][:, 1:2])
+        def fetch(t, which, lo, hi):
+            places, rate = [(n3_sb, tau3_sb), (n4_sb, tau4_sb)][which]
+            fetch_exp(eb[:, t, which, lo:hi], win2[t], places, lo, hi, rate[:, t : t + 1], bias2[t][:, which : which + 1])
 
         def subtract(t, lo, hi):
             nc.vector.tensor_tensor(gap[:, t, lo:hi], eb[:, t, 0, lo:hi], eb[:, t, 1, lo:hi], ALU.subtract)
 
-        def store_rows(ts, lo, hi):
-            nc.vector.tensor_scalar(y[:, ts, lo:hi], gap[:, ts, lo:hi], 3.0, None, ALU.mult)
-            nc.sync.dma_start(out_rows[:, ts, lo:hi], y[:, ts, lo:hi])
+        def store_rows(t, lo, hi):
+            nc.vector.tensor_scalar(y[:, t, lo:hi], gap[:, t, lo:hi], 3.0, None, ALU.mult)
+            nc.sync.dma_start(out_rows[:, t, lo:hi], y[:, t, lo:hi])
 
         def side_views(side, lo, a, b):
             return (
-                side[:, a:b, :].rearrange("p (c i) t -> p c t i", i=4),
-                gap[:, :, lo + a : lo + b].rearrange("p t (c i) -> p c t i", i=4),
+                side[:, a - lo : b - lo, :].rearrange("p (c i) t -> p c t i", i=4),
+                gap[:, :, a:b].rearrange("p t (c i) -> p c t i", i=4),
             )
 
-        mid = S // 2
-        for t in (0, 1):
-            fetch_pair(t, 0, S)
-        for lo, hi in HALVES:
-            for t in (2, 3):
-                fetch_pair(t, lo, hi)
-
-        for t in (0, 1):
-            subtract(t, 0, S)
-            store_rows(slice(t, t + 1), 0, S)
-        for lo, hi in HALVES:
-            subtract(2, lo, hi)
-            if hi == S:
-                store_rows(slice(2, 3), lo, hi)
-            subtract(3, lo, hi)
-            side = work.tile([P, hi - lo, PACK], BF16, name="y_side%d" % lo, align_bytes=64)
-            cut = TAIL_SPLIT if hi == S else mid
-            nc.vector.tensor_scalar(*side_views(side, lo, 0, cut), 3.0, None, ALU.mult)
-            if cut < mid:
-                nc.scalar.activation(*side_views(side, lo, cut, mid), ACT.Copy, scale=3.0)
-            store_rows(slice(3, 4) if hi == S else slice(2, 4), lo, hi)
+        def quantise(side, lo, hi, queue):
             nc.vector.quantize_mx(
                 out=ow[:, lo:hi].bitcast(FP8X4), scales=osc[:, lo:hi],
                 in_=side[:].rearrange("p n t -> p (n t)"),
             )
-            queue = nc.scalar if hi == S else nc.sync
             queue.dma_start(out_words[:, lo:hi], ow[:, lo:hi].bitcast(I32))
+
+        mid, last = S // 2, 3 * S // 4
+        stretches = [(0, 0, S)] + [(t, lo, hi) for lo, hi in HALVES for t in range(1, PACK)]
+        for t, lo, hi in stretches[:-1]:
+            fetch(t, 0, lo, hi)
+            fetch(t, 1, lo, hi)
+        fetch(PACK - 1, 0, mid, S)
+        fetch(PACK - 1, 1, mid, last)
+        fetch(PACK - 1, 1, last, S)
+
+        y_side = [work.tile([P, mid, PACK], BF16, name="y_side%d" % lo, align_bytes=64) for lo, hi in HALVES]
+        for t, lo, hi in stretches[:-1]:
+            subtract(t, lo, hi)
+            if (t, hi) == (PACK - 1, mid):
+                nc.vector.tensor_scalar(*side_views(y_side[0], 0, 0, mid), 3.0, None, ALU.mult)
+            store_rows(t, lo, hi)
+            if (t, hi) == (PACK - 1, mid):
+                quantise(y_side[0], 0, mid, nc.sync)
+        subtract(PACK - 1, mid, last)
+        subtract(PACK - 1, last, S)
+        nc.scalar.activation(*side_views(y_side[1], mid, mid, last), ACT.Copy, scale=3.0)
+        nc.vector.tensor_scalar(*side_views(y_side[1], mid, last, S), 3.0, None, ALU.mult)
+        nc.scalar.activation(y[:, PACK - 1, mid:S], gap[:, PACK - 1, mid:S], ACT.Copy, scale=3.0)
+        nc.scalar.dma_start(out_rows[:, PACK - 1, mid:S], y[:, PACK - 1, mid:S])
+        quantise(y_side[1], mid, S, nc.sync)
         for r in range(4):
-            queue = nc.sync if r % 2 == 0 else nc.scalar
+            queue = nc.scalar if r % 2 == 0 else nc.sync
             queue.dma_start(out_scales[r:16:4, :], osc[r:P:32, :].bitcast(I32))

from contextlib import ExitStack

import concourse.mybir as mybir

F32 = mybir.dt.float32
BF16 = mybir.dt.bfloat16
I32 = mybir.dt.int32
U32 = mybir.dt.uint32
U16 = mybir.dt.uint16
U8 = mybir.dt.uint8
FP8X4 = mybir.dt.float8_e4m3fn_x4
ALU = mybir.AluOpType
ACT = mybir.ActivationFunctionType

P = 128
PACK = 4
K, T, S, G, H = 512, 1024, 512, 2048, 512
FLOPS = 2 * 2 * K * H * S

HALVES = [(0, 256), (256, 512)]


def tile_picked_codeeosetw_none_po_kernel(
    tc, x_words, x_scales, d_words, d_scales, tau, tau2, gs, tau3, tau4,
    offs, k1, n1, n2, k2, n3, n4, out_0, out_1, out_2,
):
    nc = tc.nc
    with ExitStack() as ctx:
        keep = ctx.enter_context(tc.tile_pool(name="keep", bufs=1))
        work = ctx.enter_context(tc.tile_pool(name="work", bufs=1))
        psum = ctx.enter_context(tc.psum_pool(name="psum", bufs=1))

        def load_list(src, name):
            tile = keep.tile([P, S // 16], U16, name=name)
            nc.sync.dma_start(tile[:], src)
            return tile

        def load_rows(src, name):
            tile = keep.tile([P, PACK], F32, name=name)
            nc.gpsimd.dma_start(tile[:], src.rearrange("(p t) o -> p (t o)", t=PACK))
            return tile

        ds_tab = keep.tile([P, G], U8, name="ds_tab")
        xs_tab = keep.tile([P, T], U8, name="xs_tab")
        nc.vector.memset(ds_tab[:].bitcast(I32), 0)
        nc.vector.memset(xs_tab[:].bitcast(I32), 0)
        win1 = [keep.tile([P, 2 * S if t > 0 else S], F32, name="win1_%d" % t) for t in range(PACK)]
        win2 = [keep.tile([P, 2 * S if t == 0 else S], F32, name="win2_%d" % t) for t in range(PACK)]
        hs = [win1[1][:, S:], win1[2][:, S:], win1[3][:, S:], win2[0][:, S:]]
        k1_sb = load_list(k1, "k1_sb")
        ds_rows = d_scales[0].bitcast(I32)
        for e in range(2):
            nc.scalar.dma_start(ds_tab[e:P:16, :].bitcast(I32), ds_rows[e:16:2, :])
        offs_sb = load_list(offs, "offs_sb")
        n1_sb = load_list(n1, "n1_sb")
        n2_sb = load_list(n2, "n2_sb")
        xw_tab = keep.tile([P, T], I32, name="xw_tab")
        nc.sync.dma_start(xw_tab[:], x_words[0].rearrange("p n t -> p (n t)").bitcast(I32))
        dw_tab = keep.tile([P, G], I32, name="dw_tab")
        nc.sync.dma_start(dw_tab[:], d_words[0].rearrange("p n t -> p (n t)").bitcast(I32))
        tau_sb = load_rows(tau, "tau_sb")
        tau2_sb = load_rows(tau2, "tau2_sb")
        xs_rows = x_scales[0].bitcast(I32)
        for r in range(4):
            nc.scalar.dma_start(xs_tab[r:P:32, :].bitcast(I32), xs_rows[r:16:4, :])
        gs_sb = load_rows(gs, "gs_sb")
        tau3_sb = load_rows(tau3, "tau3_sb")
        tau4_sb = load_rows(tau4, "tau4_sb")
        k2_sb = load_list(k2, "k2_sb")
        n3_sb = load_list(n3, "n3_sb")
        n4_sb = load_list(n4, "n4_sb")

        neg12 = keep.tile([P, PACK, 2], F32, name="neg12")
        nc.scalar.activation(neg12[:, :, 0], tau_sb[:], ACT.Copy, scale=-1.0)
        nc.scalar.activation(neg12[:, :, 1], tau2_sb[:], ACT.Copy, scale=-1.0)
        neg34 = keep.tile([P, PACK, 2], F32, name="neg34")
        nc.gpsimd.tensor_scalar(neg34[:, :, 0], tau3_sb[:], -1.0, 0.0, ALU.mult, ALU.add)
        nc.gpsimd.tensor_scalar(neg34[:, :, 1], tau4_sb[:], -1.0, 0.0, ALU.mult, ALU.add)

        def pick(table, codes, dtype, tag, name):
            picked = work.tile([P, S], dtype, name=name, tag=tag, align_bytes=64)
            nc.vector.tensor_copy(picked[:], table.indirect(codes[:]))
            return picked

        def deal(dealt, picked, ts):
            nc.vector.tensor_copy(
                dealt.rearrange("p (t m) -> p m t", t=PACK)[:, :, ts],
                picked.rearrange("p (m t) -> p m t", t=PACK)[:, :, ts],
            )

        def place_scales(picked, queue, name):
            dealt = work.tile([P, H], U8, name=name, align_bytes=64)
            deal(dealt[:], picked[:], slice(0, PACK))
            for e in range(2):
                queue.dma_start(dealt[2 + e : P : 32, :].bitcast(I32), dealt[16 + e : P : 32, :].bitcast(I32))
            return dealt

        def multiply(tag, cols, t, w, ws, a, a_s):
            bank = psum.tile([P, cols.stop - cols.start], F32, name="bank", tag=tag)
            m = slice(t * P, (t + 1) * P)
            nc.tensor.matmul_mx(
                out=bank[:], lhsT=w[t].bitcast(FP8X4), lhsT_scale=ws[:, m],
                rhs=a[:, cols].bitcast(FP8X4), rhs_scale=a_s[:, cols], start=True, stop=True,
            )
            return bank, cols

        def leave_banks(parts, window, neg, name):
            tops = []
            for bank, cols in parts:
                top = work.tile([P, 1], F32, name="%s_top%d" % (name, cols.start))
                nc.vector.tensor_scalar(window[:, cols], bank[:], 0.0625, None, ALU.mult, ALU.max, accum_out=top[:])
                tops.append(top)
            bias = work.tile([P, 2], F32, name=name + "_bias")
            nc.vector.scalar_tensor_tensor(
                bias[:], tops[0][:].to_broadcast([P, 2]), tops[-1][:], neg, ALU.max, ALU.mult,
            )
            return bias

        def fetch_exp(dst, rows, places, lo, hi, rate, bias):
            nc.scalar.activation(
                dst, rows[:].indirect(places[:, lo // 16 : hi // 16]), ACT.Exp, bias=bias, scale=rate,
            )

        def halve(t):
            nc.vector.tensor_scalar(hs[t], win1[t][:, :S], gs_sb[:, t : t + 1], 0.5, ALU.mult, ALU.mult)

        dw_words = dw_tab[:].bitcast(U32)
        d1s = pick(ds_tab[:], k1_sb, U8, "scales_d", "d1s")
        w1s = place_scales(d1s, nc.sync, "w1s")
        xw = pick(xw_tab[:].bitcast(U32), offs_sb, U32, "words_x", "xw")
        d1w = pick(dw_words, k1_sb, U32, "words_d", "d1w")
        xs = pick(xs_tab[:], offs_sb, U8, "scales_x", "xs")
        d1w_by_tile = d1w[:].bitcast(I32).rearrange("p (m t) -> p m t", t=PACK)
        w1_first = work.tile([P, P], I32, name="w1_first", align_bytes=64)
        nc.vector.tensor_copy(w1_first[:], d1w_by_tile[:, :, 0])
        w1_rest = work.tile([P, PACK - 1, P], I32, name="w1_rest", align_bytes=64)
        nc.vector.tensor_copy(w1_rest[:].rearrange("p t m -> p m t"), d1w_by_tile[:, :, 1:])
        w1 = [w1_first[:]] + [w1_rest[:, t, :] for t in range(PACK - 1)]

        parts1 = [[multiply("b0%d" % lo, slice(lo, hi), 0, w1, w1s, xw, xs) for lo, hi in HALVES]]
        for t in range(1, PACK):
            parts1.append([multiply("b%d" % t, slice(0, S), t, w1, w1s, xw, xs)])
        ea = work.tile([P, PACK, 2, S], F32, name="ea")
        for t in range(PACK):
            bias = leave_banks(parts1[t], win1[t], neg12[:, t, :], "h%d" % t)
            if t > 0:
                halve(t - 1)
            cuts = HALVES if t == 0 else [(0, S)]
            for lo, hi in cuts:
                fetch_exp(ea[:, t, 1, lo:hi], win1[t], n2_sb, lo, hi, tau2_sb[:, t : t + 1], bias[:, 1:2])
            for lo, hi in cuts:
                fetch_exp(ea[:, t, 0, lo:hi], win1[t], n1_sb, lo, hi, tau_sb[:, t : t + 1], bias[:, 0:1])

        d2s = pick(ds_tab[:], k2_sb, U8, "scales_x", "d2s")
        d2w = pick(dw_words, k2_sb, U32, "words_x", "d2w")
        w2s = place_scales(d2s, nc.sync, "w2s")
        w2_all = work.tile([P, H], I32, name="w2_all", align_bytes=64)
        deal(w2_all[:], d2w[:].bitcast(I32), slice(0, PACK))
        w2 = [w2_all[:, t * P : (t + 1) * P] for t in range(PACK)]

        halve(PACK - 1)

        zs = work.tile([P, S], U8, name="zs", align_bytes=64)
        parts2 = [[]]
        below = work.tile([P, S], F32, name="below")
        nc.vector.tensor_scalar(below[:], ea[:, 0, 1, :], 0.25, None, ALU.add)
        inverse = work.tile([P, S], F32, name="inverse", tag="logs")
        nc.vector.reciprocal(inverse[:], below[:])
        ratio = work.tile([P, S], F32, name="ratio")
        nc.vector.scalar_tensor_tensor(ratio[:], ea[:, 0, 0, :], 0.25, inverse[:], ALU.add, ALU.mult)

        units = [HALVES[0] + (t,) for t in (0, 1, 2, 3)] + [HALVES[1] + (t,) for t in (1, 2, 3, 0)]
        logs = work.tile([P, len(units), 2, S // 2], F32, name="logs", tag="logs")
        diff = work.tile([P, len(units), S // 2], F32, name="diff")
        z_rows = [work.tile([P, PACK, S // 2], BF16, name="z_rows%d" % lo, tag="z_rows%d" % lo, align_bytes=64) for lo, hi in HALVES]
        for u, (lo, hi, t) in enumerate(units):
            if t == 0:
                nc.scalar.activation(diff[:, u, :], ratio[:, lo:hi], ACT.Ln)
            else:
                nc.scalar.activation(logs[:, u, :, :], ea[:, t, :, lo:hi], ACT.Ln, bias=0.25)

        def weigh(u):
            lo, hi, t = units[u]
            nc.vector.scalar_tensor_tensor(
                z_rows[u // PACK][:, t, :], diff[:, u, :], gs_sb[:, t : t + 1], hs[t][:, lo:hi], ALU.mult, ALU.add,
            )

        weigh(0)
        for u in range(1, len(units) - 1):
            nc.vector.tensor_tensor(diff[:, u, :], logs[:, u, 0, :], logs[:, u, 1, :], ALU.subtract)
            if u > 1:
                weigh(u - 1)
        weigh(len(units) - 2)
        weigh(len(units) - 1)
        z_side = [work.tile([P, S // 2, PACK], BF16, name="z_side%d" % lo, align_bytes=64) for lo, hi in HALVES]
        for c, copy in enumerate([nc.scalar.copy, nc.vector.tensor_copy]):
            copy(
                z_side[c][:].rearrange("p (c i) t -> p c t i", i=4),
                z_rows[c][:].rearrange("p t (c i) -> p c t i", i=4),
            )
        zw = work.tile([P, S], U32, name="zw", tag="z_rows256", align_bytes=64)
        for c, (lo, hi) in enumerate(HALVES):
            nc.vector.quantize_mx(
                out=zw[:, lo:hi].bitcast(FP8X4), scales=zs[:, lo:hi],
                in_=z_side[c][:].rearrange("p n t -> p (n t)"),
            )
            parts2[0].append(multiply("b0%d" % lo, slice(lo, hi), 0, w2, w2s, zw, zs))
        for t in range(1, PACK):
            parts2.append([multiply("b%d" % t, slice(0, S), t, w2, w2s, zw, zs)])

        bias2 = [leave_banks(parts2[t], win2[t], neg34[:, t, :], "g%d" % t) for t in range(PACK)]
        ow = work.tile([P, S], U32, name="ow", align_bytes=64)
        osc = work.tile([P, S], U8, name="osc", align_bytes=64)
        out_rows = out_0.rearrange("(p t) j -> p t j", t=PACK)
        out_words = out_1[0].rearrange("p n t -> p (n t)").bitcast(I32)
        out_scales = out_2[0].bitcast(I32)
        eb = work.tile([P, PACK, 2, S], F32, name="eb")
        gap = work.tile([P, PACK, S], F32, name="gap")
        y = work.tile([P, PACK, S], F32, name="y")

        def fetch(t, which, lo, hi):
            places, rate = [(n3_sb, tau3_sb), (n4_sb, tau4_sb)][which]
            fetch_exp(eb[:, t, which, lo:hi], win2[t], places, lo, hi, rate[:, t : t + 1], bias2[t][:, which : which + 1])

        def subtract(t, lo, hi):
            nc.vector.tensor_tensor(gap[:, t, lo:hi], eb[:, t, 0, lo:hi], eb[:, t, 1, lo:hi], ALU.subtract)

        def store_rows(t, lo, hi):
            nc.vector.tensor_scalar(y[:, t, lo:hi], gap[:, t, lo:hi], 3.0, None, ALU.mult)
            nc.sync.dma_start(out_rows[:, t, lo:hi], y[:, t, lo:hi])

        def side_views(side, lo, a, b):
            return (
                side[:, a - lo : b - lo, :].rearrange("p (c i) t -> p c t i", i=4),
                gap[:, :, a:b].rearrange("p t (c i) -> p c t i", i=4),
            )

        def quantise(side, lo, hi, queue):
            nc.vector.quantize_mx(
                out=ow[:, lo:hi].bitcast(FP8X4), scales=osc[:, lo:hi],
                in_=side[:].rearrange("p n t -> p (n t)"),
            )
            queue.dma_start(out_words[:, lo:hi], ow[:, lo:hi].bitcast(I32))

        mid, last = S // 2, 3 * S // 4
        stretches = [(0, 0, S)] + [(t, lo, hi) for lo, hi in HALVES for t in range(1, PACK)]
        for t, lo, hi in stretches[:-1]:
            fetch(t, 0, lo, hi)
            fetch(t, 1, lo, hi)
        fetch(PACK - 1, 0, mid, S)
        fetch(PACK - 1, 1, mid, last)
        fetch(PACK - 1, 1, last, S)

        y_side = [work.tile([P, mid, PACK], BF16, name="y_side%d" % lo, align_bytes=64) for lo, hi in HALVES]
        for t, lo, hi in stretches[:-1]:
            subtract(t, lo, hi)
            if (t, hi) == (PACK - 1, mid):
                nc.vector.tensor_scalar(*side_views(y_side[0], 0, 0, mid), 3.0, None, ALU.mult)
            store_rows(t, lo, hi)
            if (t, hi) == (PACK - 1, mid):
                quantise(y_side[0], 0, mid, nc.sync)
        subtract(PACK - 1, mid, last)
        subtract(PACK - 1, last, S)
        nc.scalar.activation(*side_views(y_side[1], mid, mid, last), ACT.Copy, scale=3.0)
        nc.vector.tensor_scalar(*side_views(y_side[1], mid, last, S), 3.0, None, ALU.mult)
        nc.scalar.activation(y[:, PACK - 1, mid:S], gap[:, PACK - 1, mid:S], ACT.Copy, scale=3.0)
        nc.scalar.dma_start(out_rows[:, PACK - 1, mid:S], y[:, PACK - 1, mid:S])
        quantise(y_side[1], mid, S, nc.sync)
        for r in range(4):
            queue = nc.scalar if r % 2 == 0 else nc.sync
            queue.dma_start(out_scales[r:16:4, :], osc[r:P:32, :].bitcast(I32))
